import numpy as np
import ml_dtypes


def mxq(x, axis, fmt="e4m3"):
    dtype, down = {"e4m3": (ml_dtypes.float8_e4m3fn, 7), "e5m2": (ml_dtypes.float8_e5m2, 14)}[fmt]
    v = np.moveaxis(np.asarray(x, np.float32).astype(ml_dtypes.bfloat16).astype(np.float64), axis, -1)
    blocks = v.reshape(v.shape[:-1] + (-1, 32))
    amax = np.abs(blocks).max(-1, keepdims=True)
    byte = np.maximum(np.where(amax > 0, np.frexp(amax)[1] - 1 + 127, 0) - down, 1)
    scale = np.exp2(byte - 127.0)
    codes = (blocks / scale).astype(np.float32).astype(dtype).astype(np.float64)
    return np.moveaxis((codes * scale).reshape(v.shape), -1, axis)


WIDE = False


def mx_kscale(k):
    if not WIDE:
        return np.ones(k)
    levels = np.array([10, -10, 5, -5, 0])
    if k % 512:
        return np.exp2(np.random.permutation(np.resize(levels, k // 32))).repeat(32)
    a = np.empty((k // 512, 16))
    for p in range(k // 512):
        a[p, :8] = np.random.permutation(np.resize(levels, 8))
        for g in range(8):
            far = levels[np.abs(levels - a[p, g]) >= 10]
            a[p, g + 8] = far[np.random.randint(len(far))]
    return np.exp2(a.ravel()).repeat(32)


def f64(x):
    return np.asarray(x).astype(np.float64)


def striped(idx):
    return np.tile(idx.reshape(-1, 16).T, (8, 1)).astype(np.uint16)


def unstriped(offs):
    return offs[:16].T.reshape(-1).astype(np.int64)


E2M1 = np.array([0.0, 0.5, 1.0, 1.5, 2.0, 3.0, 4.0, 6.0, -0.0, -0.5, -1.0, -1.5, -2.0, -3.0, -4.0, -6.0])


def pack_weight(w, fmt):
    k, n = w.shape
    w = f64(np.asarray(w, np.float32).astype(ml_dtypes.bfloat16)).reshape(k // 32, 32, n)
    amax = np.abs(w).max(1)
    if fmt == "e4m3":
        byte = np.frexp(amax)[1] - 1 + 127 - 7
    else:
        mant, ex = np.frexp(amax / 6.0)
        byte = np.where(mant > 0.5, ex, ex - 1) + 127
    byte = np.clip(np.where(amax > 0, byte, 1), 1, 254)
    scaled = (w * np.exp2(127.0 - byte)[:, None, :]).reshape(k, n).astype(np.float32)
    by_word = np.ascontiguousarray(scaled.reshape(k // 512, 128, 4, n).transpose(0, 1, 3, 2))
    if fmt == "e4m3":
        words = by_word.astype(ml_dtypes.float8_e4m3fn).view(np.uint8)
    else:
        c = by_word.astype(ml_dtypes.float4_e2m1fn).view(np.uint8) & 0xF
        words = (c[..., 0::2] | (c[..., 1::2] << 4)).reshape(k // 512, 128, 2 * n)
    return np.ascontiguousarray(words), np.ascontiguousarray(byte.astype(np.uint8).reshape(k // 512, 16, n))


def unpack_weight(words, scales, fmt):
    g, _, n = scales.shape
    words = np.ascontiguousarray(words).reshape(g, 128, n, -1)
    if fmt == "e4m3":
        vals = words.view(ml_dtypes.float8_e4m3fn).astype(np.float64)
    else:
        nib = np.empty((g, 128, n, 4), np.uint8)
        nib[..., 0::2] = words & 0xF
        nib[..., 1::2] = words >> 4
        vals = E2M1[nib]
    vals = vals * np.repeat(np.exp2(scales.astype(np.float64) - 127.0), 8, axis=1)[..., None]
    return vals.transpose(0, 1, 3, 2).reshape(g * 512, n)


def gelu(v):
    return 0.5 * v * (1.0 + np.tanh(np.sqrt(2.0 / np.pi) * (v + 0.044715 * v**3)))


def bf(x):
    return np.asarray(x, np.float32).astype(ml_dtypes.bfloat16)


def planes(Y):
    n, m = Y.shape
    b = f64(bf(Y)).reshape(n // 32, 32, m)
    amax = np.abs(b).max(1)
    byte = np.clip(np.where(amax > 0, np.frexp(amax)[1] - 1 + 127 - 7, 1), 1, 254)
    codes = (b * np.exp2(127.0 - byte)[:, None, :]).reshape(n, m).astype(np.float32).astype(ml_dtypes.float8_e4m3fn).view(np.uint8)
    words = codes.reshape(n // 512, 128, 4, m).transpose(0, 1, 3, 2)
    return np.ascontiguousarray(words), np.ascontiguousarray(byte.astype(np.uint8).reshape(n // 512, 16, m))


K, H, N, T, S, P, P2 = 1024, 512, 1024, 4096, 1024, 512, 256

def setup_inputs():
    n = np.random.standard_normal
    s, u = mx_kscale(K)[:, None], mx_kscale(H)[:, None]
    tab_words, tab_scales = pack_weight(n((K, T)) * s, "e4m3")
    w3_words, w3_scales = pack_weight(1.3 * n((K, H)) / np.sqrt(K) / s, "e2m1")
    w4 = 0.7 * n((H, N)) * np.exp(0.8 * n(N)) / np.sqrt(H) / u
    w4_words, w4_scales = pack_weight(w4, "e4m3")
    sides = np.random.permutation(S)
    return {
        "tab_words": tab_words, "tab_scales": tab_scales,
        "offs": striped(np.random.permutation(T)[:S]),
        "w1": (n((K, H)) / np.sqrt(K) / s).astype(np.float32),
        "w2": (n((K, H)) / np.sqrt(K) / s).astype(np.float32),
        "w3_words": w3_words, "w3_scales": w3_scales,
        "gain": (np.exp(0.3 * n(H)) * u[:, 0]).astype(np.float32),
        "pos1": striped(sides[:P]), "pos2": striped(sides[-P:]),
        "w4_words": w4_words, "w4_scales": w4_scales,
        "pos3": striped(np.random.permutation(P)[:P2]),
        "pos4": striped(np.random.permutation(P)[:P2]),
    }

def reference(tab_words, tab_scales, offs, w1, w2, w3_words, w3_scales, gain, pos1, pos2, w4_words, w4_scales, pos3, pos4):
    v = unpack_weight(tab_words, tab_scales, "e4m3")[:, unstriped(offs)]
    a1 = mxq(f64(w1), 0, "e4m3").T @ v
    a2 = mxq(f64(w2), 0, "e4m3").T @ v
    a3 = unpack_weight(w3_words, w3_scales, "e2m1").T @ v
    h = (np.maximum(a1, a2) + np.tanh(a3)) * f64(gain)[:, None]
    z = h[:, unstriped(pos1)] - h[:, unstriped(pos2)]
    f = unpack_weight(w4_words, w4_scales, "e4m3").T @ mxq(z, 0, "e4m3")
    y = f[:, unstriped(pos3)] * np.tanh(f[:, unstriped(pos4)])
    words, scales = planes(y)
    return y, words, scales

@@ -1,0 +1,282 @@
+from contextlib import ExitStack
+
+import concourse.mybir as mybir
+from concourse.masks import make_identity
+
+K, H, N, T, S, M1, M2 = 1024, 512, 1024, 4096, 1024, 512, 256
+FLOPS = 2 * (3 * K * H * S + H * N * M1)
+
+F32 = mybir.dt.float32
+BF16 = mybir.dt.bfloat16
+I32 = mybir.dt.int32
+U32 = mybir.dt.uint32
+U16 = mybir.dt.uint16
+U8 = mybir.dt.uint8
+FP8X4 = mybir.dt.float8_e4m3fn_x4
+FP4X4 = mybir.dt.float4_e2m1fn_x4
+ALU = mybir.AluOpType
+ACT = mybir.ActivationFunctionType
+
+P = 128
+PACK = 4
+KP = P * PACK
+PASSES = K // KP
+BANK = 512
+QUADS = 4
+
+
+def tile_list_canopy_berry_walk_kernel(
+    tc, tab_words, tab_scales, offs, w1, w2, w3_words, w3_scales, gain,
+    pos1, pos2, w4_words, w4_scales, pos3, pos4, out_0, out_1, out_2,
+):
+    nc = tc.nc
+    with ExitStack() as ctx:
+        lists = ctx.enter_context(tc.tile_pool(name="lists", bufs=1))
+        sbuf = ctx.enter_context(tc.tile_pool(name="sbuf", bufs=1))
+        psum = ctx.enter_context(tc.psum_pool(name="psum", bufs=1))
+
+        def tile(name, shape, dtype, bufs=1):
+            return sbuf.tile(shape, dtype, name=name, bufs=bufs, align_bytes=64)
+
+        def bank(b):
+            return psum.tile([P, BANK], F32, name="bank%d" % b)
+
+        def load_list(name, src):
+            dst = lists.tile(list(src.shape), U16, name=name)
+            nc.sync.dma_start(dst[:], src)
+            return dst
+
+        idx = load_list("idx", offs)
+
+        w3 = tile("w3", [P, PASSES, 2 * H], U8)
+        nc.sync.dma_start(out=w3[:].bitcast(I32), in_=w3_words.rearrange("a p c -> p a c").bitcast(I32))
+        tab_sc = tile("tab_sc", [P, T], U8)
+        nc.vector.memset(tab_sc[:].bitcast(I32), 0)
+        for q in range(QUADS):
+            nc.sync.dma_start(
+                out=tab_sc[32 * q : 32 * q + 8, :].bitcast(I32),
+                in_=tab_scales[:, 4 * q : 4 * q + 4, :].bitcast(I32),
+            )
+
+        w3_sc = tile("w3_sc", [P, PASSES, H], U8)
+        nc.gpsimd.memset(w3_sc[:].bitcast(I32), 0)
+        for q in range(QUADS):
+            nc.gpsimd.dma_start(
+                out=w3_sc[32 * q : 32 * q + 4].bitcast(I32),
+                in_=w3_scales[:, 4 * q : 4 * q + 4, :].rearrange("a r c -> r a c").bitcast(I32),
+            )
+        v_sc_last = tile("v_sc_last", [P, S], U8)
+        nc.gpsimd.memset(v_sc_last[:].bitcast(I32), 0)
+        ident = tile("ident", [P, P], F32)
+        make_identity(nc, ident[:])
+        w4_sc_raw = tile("w4_sc_raw", [P, N], U8)
+        nc.gpsimd.memset(w4_sc_raw[:].bitcast(I32), 0)
+
+        tab = [tile("tab%d" % a, [P, T], I32) for a in range(PASSES)]
+
+        def load_tab(a):
+            nc.sync.dma_start(out=tab[a][:], in_=tab_words[a].rearrange("p c i -> p (c i)").bitcast(I32))
+
+        load_tab(0)
+        load_tab(1)
+
+        def load_w(name, w, a, parts):
+            width = H // parts
+            rows = w[KP * a : KP * (a + 1), :].rearrange("(p j) c -> p j c", j=PACK)
+            raws = []
+            for h in range(parts):
+                raw = tile("%s_raw%d_%d" % (name, a, h), [P, PACK, width], F32)
+                nc.sync.dma_start(out=raw[:], in_=rows[:, :, width * h : width * (h + 1)])
+                raws.append(raw)
+            return raws
+
+        w1_raw = [load_w("w1", w1, a, 1) for a in range(PASSES)]
+        w2_raw = [load_w("w2", w2, 0, 1), load_w("w2", w2, 1, 2)]
+        gain_sb = tile("gain_sb", [P, PACK], F32)
+        nc.sync.dma_start(out=gain_sb[:], in_=gain.rearrange("(p t) -> p t", t=PACK))
+        p1 = load_list("p1", pos1)
+        p2 = load_list("p2", pos2)
+        w4_raw = tile("w4_raw", [P, N], I32)
+        nc.sync.dma_start(out=w4_raw[:], in_=w4_words[0].rearrange("p c i -> p (c i)").bitcast(I32))
+        for q in range(QUADS):
+            nc.sync.dma_start(
+                out=w4_sc_raw[32 * q : 32 * q + 4, :].bitcast(I32),
+                in_=w4_scales[0, 4 * q : 4 * q + 4, :].bitcast(I32),
+            )
+        p3 = load_list("p3", pos3)
+        p4 = load_list("p4", pos4)
+
+        v_sc = tile("v_sc", [P, S], U8)
+        nc.vector.tensor_copy(out=v_sc[:], in_=tab_sc[:].indirect(idx[:]))
+        nc.gpsimd.dma_start(out=v_sc_last[0:100, :].bitcast(I32), in_=v_sc[4:104, :].bitcast(I32))
+        half_cols = S // 2 // 16
+        v = []
+        for a in range(PASSES):
+            halves = []
+            for h in range(2):
+                vh = tile("v%d_%d" % (a, h), [P, S // 2], U32)
+                nc.vector.tensor_copy(
+                    out=vh[:], in_=tab[a][:].bitcast(U32).indirect(idx[:, half_cols * h : half_cols * (h + 1)])
+                )
+                halves.append(vh)
+            v.append(halves)
+
+        def v_words(a, jt):
+            return v[a][jt // 4][:, P * (jt % 4) : P * (jt % 4 + 1)].bitcast(FP8X4)
+
+        def v_plane(a, jt):
+            return v_sc[4 * a :, P * jt : P * (jt + 1)]
+
+        jts = S // P
+        a3 = [bank(jt) for jt in range(jts)]
+        for a in range(PASSES):
+            plane = v_sc if a == 0 else v_sc_last
+            for jt in range(jts):
+                nc.tensor.matmul_mx(
+                    out=a3[jt][:], lhsT=v_words(a, jt), lhsT_scale=plane[:, P * jt : P * (jt + 1)],
+                    rhs=w3[:, a, :].bitcast(FP4X4), rhs_scale=w3_sc[:, a, :],
+                    start=(a == 0), stop=(a == PASSES - 1),
+                )
+        tanh3 = []
+        for jt in range(jts):
+            th = tile("tanh3_%d" % jt, [P, PACK, P], F32)
+            nc.scalar.activation(out=th[:], in_=a3[jt][:].rearrange("p (q t) -> p t q", t=PACK), func=ACT.Tanh)
+            tanh3.append(th)
+
+        def quantise_w(name, a, raws, slices):
+            grouped = tile("w_bf16", [P, PACK, P, PACK], BF16, bufs=2)
+            qs = P // len(raws)
+            for h, raw in enumerate(raws):
+                nc.vector.tensor_copy(
+                    out=grouped[:, :, qs * h : qs * (h + 1), :].rearrange("p t q j -> p q j t"),
+                    in_=raw[:].rearrange("p j (q t) -> p q j t", t=PACK),
+                )
+            codes = tile("%s_codes%d" % (name, a), [P, H], U32)
+            scales = tile("%s_sc%d" % (name, a), [P, H], U8)
+            ts = PACK // slices
+            for s in range(slices):
+                cols = slice(P * ts * s, P * ts * (s + 1))
+                nc.vector.quantize_mx(
+                    out=codes[:, cols].bitcast(FP8X4), scales=scales[:, cols],
+                    in_=grouped[:, ts * s : ts * (s + 1)].rearrange("p t q j -> p (t q j)"),
+                )
+            return codes, scales
+
+        w1_q = [quantise_w("w1", a, w1_raw[a], 2) for a in range(PASSES)]
+
+        def product(dst, wq, jt0, count, cols):
+            width = BANK // count
+            for a in range(PASSES):
+                for k in range(count):
+                    nc.tensor.matmul_mx(
+                        out=dst[:, width * k : width * (k + 1)],
+                        lhsT=v_words(a, jt0 + k), lhsT_scale=v_plane(a, jt0 + k),
+                        rhs=wq[a][0][:, cols].bitcast(FP8X4), rhs_scale=wq[a][1][:, cols],
+                        start=(a == 0 and k == 0), stop=(a == PASSES - 1 and k == count - 1),
+                    )
+
+        def first_product(u):
+            a1u = tile("a1_%d" % u, [P, 2, jts, P], F32)
+            for jj in range(4):
+                acc = bank(4 * u + jj)
+                product(acc, w1_q, 2 * jj, 2, slice(2 * P * u, 2 * P * (u + 1)))
+                nc.scalar.copy(
+                    out=a1u[:, :, 2 * jj : 2 * jj + 2, :],
+                    in_=acc[:].rearrange("p (k t q) -> p t k q", k=2, t=2),
+                )
+            return a1u
+
+        a1 = first_product(0)
+
+        w2_q = [quantise_w("w2", 0, w2_raw[0], 1), quantise_w("w2", 1, w2_raw[1], 4)]
+
+        w4 = tile("w4", [P, 2, PACK, P], I32)
+        w4_sc = tile("w4_sc", [P, 2, PACK, P], U8)
+
+        def deal_w4():
+            nc.vector.tensor_copy(
+                out=w4[:].rearrange("p g t q -> p g q t"),
+                in_=w4_raw[:].rearrange("p (g q t) -> p g q t", g=2, t=PACK),
+            )
+            nc.vector.tensor_copy(
+                out=w4_sc[:].rearrange("p g t q -> p g q t"),
+                in_=w4_sc_raw[:].rearrange("p (g q t) -> p g q t", g=2, t=PACK),
+            )
+
+        z = [tile("z%d" % h, [P, PACK, M1 // 2], F32) for h in range(2)]
+        for t in range(PACK):
+            if t == 2:
+                a1 = first_product(1)
+            first_bank = 4 if t in (0, 3) else 0
+            h_t = tile("h", [P, S], F32, bufs=3)
+            for h in range(2):
+                acc = bank(first_bank + h)
+                product(acc, w2_q, 4 * h, 4, slice(P * t, P * (t + 1)))
+                top = tile("top", [P, 4, P], F32, bufs=4)
+                nc.vector.tensor_tensor(
+                    out=top[:], in0=acc[:].rearrange("p (k q) -> p k q", k=4),
+                    in1=a1[:, t % 2, 4 * h : 4 * h + 4, :], op=ALU.max,
+                )
+                turned = bank(first_bank + 2 + h)
+                for k in range(4):
+                    cols = slice(P * k, P * (k + 1))
+                    nc.tensor.matmul(turned[:, cols], tanh3[4 * h + k][:, t, :], ident[:],
+                                     start=True, stop=False, is_transpose=True)
+                    nc.tensor.matmul(turned[:, cols], top[:, k, :], ident[:],
+                                     start=False, stop=True, is_transpose=True)
+                nc.scalar.activation(out=h_t[:, BANK * h : BANK * (h + 1)], in_=turned[:], func=ACT.Copy,
+                                     scale=gain_sb[:, t : t + 1])
+            if t == 0:
+                deal_w4()
+            shade = tile("shade", [P, M1], F32, bufs=2)
+            nc.vector.tensor_copy(out=shade[:], in_=h_t[:].indirect(p2[:]))
+            for h in range(2):
+                nc.vector.tensor_tensor(
+                    out=z[h][:, t, :], in0=h_t[:].indirect(p1[:, 16 * h : 16 * (h + 1)]),
+                    in1=shade[:, 256 * h : 256 * (h + 1)], op=ALU.subtract,
+                )
+
+        def interleave(copy, name, src):
+            width = src.shape[2]
+            dst = tile(name, [P, width, PACK], BF16)
+            copy(out=dst[:].rearrange("p (c i) t -> p c t i", i=4), in_=src[:].rearrange("p t (c i) -> p c t i", i=4))
+            return dst
+
+        z_codes = tile("z_codes", [P, M1], U32)
+        z_sc = tile("z_sc", [P, M1], U8)
+        zb = [interleave(nc.scalar.copy, "zb0", z[0]), interleave(nc.vector.tensor_copy, "zb1", z[1])]
+        for h in range(2):
+            cols = slice(256 * h, 256 * (h + 1))
+            nc.vector.quantize_mx(out=z_codes[:, cols].bitcast(FP8X4), scales=z_sc[:, cols],
+                                  in_=zb[h][:].rearrange("p m t -> p (m t)"))
+
+        y_rows = out_0.rearrange("(g p t) j -> g p t j", g=2, t=PACK)
+        y_sc = tile("y_sc", [P, 2, M2], U8)
+        for g in range(2):
+            y = tile("y%d" % g, [P, PACK, M2], F32)
+            for t in range(PACK):
+                acc = bank(4 * g + t)
+                nc.tensor.matmul_mx(
+                    out=acc[:], lhsT=w4[:, g, t, :].bitcast(FP8X4), lhsT_scale=w4_sc[:, g, t, :],
+                    rhs=z_codes[:].bitcast(FP8X4), rhs_scale=z_sc[:], start=True, stop=True,
+                )
+                f = tile("f", [P, M1], F32, bufs=4)
+                nc.scalar.copy(out=f[:], in_=acc[:])
+                other = tile("other", [P, M2], F32, bufs=3)
+                nc.vector.tensor_copy(out=other[:], in_=f[:].indirect(p4[:]))
+                bounded = tile("bounded", [P, M2], F32, bufs=3)
+                nc.scalar.activation(out=bounded[:], in_=other[:], func=ACT.Tanh)
+                nc.vector.tensor_tensor(out=y[:, t, :], in0=f[:].indirect(p3[:]), in1=bounded[:], op=ALU.mult)
+                if t % 2 == 1:
+                    nc.sync.dma_start(out=y_rows[g, :, t - 1 : t + 1, :], in_=y[:, t - 1 : t + 1, :])
+            yb = interleave(nc.scalar.copy if g == 0 else nc.vector.tensor_copy, "yb%d" % g, y)
+            y_codes = tile("y_codes%d" % g, [P, M2], I32)
+            nc.vector.quantize_mx(out=y_codes[:].bitcast(FP8X4), scales=y_sc[:, g, :],
+                                  in_=yb[:].rearrange("p m t -> p (m t)"))
+            nc.sync.dma_start(out=out_1[g].rearrange("p m i -> p (m i)").bitcast(I32), in_=y_codes[:])
+        for q in range(QUADS):
+            queue = nc.scalar if q % 2 == 0 else nc.sync
+            queue.dma_start(
+                out=out_2[:, 4 * q : 4 * q + 4, :].rearrange("g r m -> r g m").bitcast(I32),
+                in_=y_sc[32 * q : 32 * q + 4].bitcast(I32),
+            )

@@ -46,69 +46,52 @@ def tile_list_canopy_berry_walk_kernel(
             nc.sync.dma_start(dst[:], src)
             return dst
 
-        idx = load_list("idx", offs)
-
         w3 = tile("w3", [P, PASSES, 2 * H], U8)
         nc.sync.dma_start(out=w3[:].bitcast(I32), in_=w3_words.rearrange("a p c -> p a c").bitcast(I32))
-        tab_sc = tile("tab_sc", [P, T], U8)
-        nc.vector.memset(tab_sc[:].bitcast(I32), 0)
-        for q in range(QUADS):
-            nc.sync.dma_start(
-                out=tab_sc[32 * q : 32 * q + 8, :].bitcast(I32),
-                in_=tab_scales[:, 4 * q : 4 * q + 4, :].bitcast(I32),
-            )
-
-        w3_sc = tile("w3_sc", [P, PASSES, H], U8)
-        nc.gpsimd.memset(w3_sc[:].bitcast(I32), 0)
-        for q in range(QUADS):
-            nc.gpsimd.dma_start(
-                out=w3_sc[32 * q : 32 * q + 4].bitcast(I32),
-                in_=w3_scales[:, 4 * q : 4 * q + 4, :].rearrange("a r c -> r a c").bitcast(I32),
-            )
-        v_sc_last = tile("v_sc_last", [P, S], U8)
-        nc.gpsimd.memset(v_sc_last[:].bitcast(I32), 0)
-        ident = tile("ident", [P, P], F32)
-        make_identity(nc, ident[:])
-        w4_sc_raw = tile("w4_sc_raw", [P, N], U8)
-        nc.gpsimd.memset(w4_sc_raw[:].bitcast(I32), 0)
-
-        tab = [tile("tab%d" % a, [P, T], I32) for a in range(PASSES)]
-
-        def load_tab(a):
-            nc.sync.dma_start(out=tab[a][:], in_=tab_words[a].rearrange("p c i -> p (c i)").bitcast(I32))
-
-        load_tab(0)
-        load_tab(1)
-
-        def load_w(name, w, a, parts):
-            width = H // parts
-            rows = w[KP * a : KP * (a + 1), :].rearrange("(p j) c -> p j c", j=PACK)
-            raws = []
-            for h in range(parts):
-                raw = tile("%s_raw%d_%d" % (name, a, h), [P, PACK, width], F32)
-                nc.sync.dma_start(out=raw[:], in_=rows[:, :, width * h : width * (h + 1)])
-                raws.append(raw)
-            return raws
-
-        w1_raw = [load_w("w1", w1, a, 1) for a in range(PASSES)]
-        w2_raw = [load_w("w2", w2, 0, 1), load_w("w2", w2, 1, 2)]
-        gain_sb = tile("gain_sb", [P, PACK], F32)
-        nc.sync.dma_start(out=gain_sb[:], in_=gain.rearrange("(p t) -> p t", t=PACK))
+        idx = load_list("idx", offs)
         p1 = load_list("p1", pos1)
         p2 = load_list("p2", pos2)
-        w4_raw = tile("w4_raw", [P, N], I32)
-        nc.sync.dma_start(out=w4_raw[:], in_=w4_words[0].rearrange("p c i -> p (c i)").bitcast(I32))
-        for q in range(QUADS):
-            nc.sync.dma_start(
-                out=w4_sc_raw[32 * q : 32 * q + 4, :].bitcast(I32),
-                in_=w4_scales[0, 4 * q : 4 * q + 4, :].bitcast(I32),
-            )
         p3 = load_list("p3", pos3)
         p4 = load_list("p4", pos4)
+        gain_sb = tile("gain_sb", [P, PACK], F32)
+        nc.sync.dma_start(out=gain_sb[:], in_=gain.rearrange("(p t) -> p t", t=PACK))
 
-        v_sc = tile("v_sc", [P, S], U8)
-        nc.vector.tensor_copy(out=v_sc[:], in_=tab_sc[:].indirect(idx[:]))
-        nc.gpsimd.dma_start(out=v_sc_last[0:100, :].bitcast(I32), in_=v_sc[4:104, :].bitcast(I32))
+        tab_sc = tile("stage_a", [P, T], U8)
+        nc.vector.memset(tab_sc[:].bitcast(I32), 0)
+        nc.scalar.dma_start(
+            out=tab_sc[0:P:4, :].bitcast(I32), in_=tab_scales.rearrange("a x c -> x a c").bitcast(I32)
+        )
+        v_sc = tile("v_sc", [P, PASSES, S], U8)
+        nc.vector.memset(v_sc[:].bitcast(I32), 0)
+
+        def load_scale_rows(name, src):
+            dst = tile(name, [P, src.shape[0], src.shape[2]], U8)
+            nc.gpsimd.memset(dst[:].bitcast(I32), 0)
+            for q in range(QUADS):
+                nc.gpsimd.dma_start(
+                    out=dst[32 * q : 32 * q + 4].bitcast(I32),
+                    in_=src[:, 4 * q : 4 * q + 4, :].rearrange("a r c -> r a c").bitcast(I32),
+                )
+            return dst
+
+        w3_sc = load_scale_rows("w3_sc", w3_scales)
+        w4_sc_raw = load_scale_rows("w4_sc_raw", w4_scales)
+        ident = tile("ident", [P, P], F32)
+        make_identity(nc, ident[:])
+
+        tab = []
+        for a, name in enumerate(("stage_b", "stage_c")):
+            words = tile(name, [P, T], I32)
+            nc.sync.dma_start(out=words[:], in_=tab_words[a].rearrange("p c i -> p (c i)").bitcast(I32))
+            tab.append(words)
+
+        picked_sc = tile("picked_sc", [P, S], U8)
+        nc.vector.tensor_copy(out=picked_sc[:], in_=tab_sc[:].indirect(idx[:]))
+        for q in range(QUADS):
+            nc.sync.dma_start(
+                out=v_sc[32 * q : 32 * q + 4].bitcast(I32),
+                in_=picked_sc[32 * q : 32 * q + 32 : 4, :].bitcast(I32),
+            )
         half_cols = S // 2 // 16
         v = []
         for a in range(PASSES):
@@ -125,116 +108,71 @@ def tile_list_canopy_berry_walk_kernel(
             return v[a][jt // 4][:, P * (jt % 4) : P * (jt % 4 + 1)].bitcast(FP8X4)
 
         def v_plane(a, jt):
-            return v_sc[4 * a :, P * jt : P * (jt + 1)]
+            return v_sc[:, a, P * jt : P * (jt + 1)]
+
+        def quantise_w(name, w, a, stages):
+            rows = w[KP * a : KP * (a + 1), :].rearrange("(p j) c -> p j c", j=PACK)
+            grouped = tile("w_bf16", [P, 2, PACK, P // 2, PACK], BF16, bufs=2)
+            codes = tile("%s_codes%d" % (name, a), [P, H], U32)
+            scales = tile("%s_sc%d" % (name, a), [P, H], U8)
+            width = H // len(stages)
+            us = 2 // len(stages)
+            for s, stage in enumerate(stages):
+                cols = slice(width * s, width * (s + 1))
+                raw = tile(stage, [P, PACK, width], F32)
+                nc.sync.dma_start(out=raw[:], in_=rows[:, :, cols])
+                part = grouped[:, us * s : us * (s + 1)]
+                nc.vector.tensor_copy(
+                    out=part.rearrange("p u t q j -> p u q j t"),
+                    in_=raw[:].rearrange("p j (u q t) -> p u q j t", u=us, t=PACK),
+                )
+                nc.vector.quantize_mx(
+                    out=codes[:, cols].bitcast(FP8X4), scales=scales[:, cols],
+                    in_=part.rearrange("p u t q j -> p (u t q j)"),
+                )
+            return codes[:].bitcast(FP8X4), scales[:]
+
+        w3_q = [(w3[:, a, :].bitcast(FP4X4), w3_sc[:, a, :]) for a in range(PASSES)]
+        w1_q = [quantise_w("w1", w1, 0, ["stage_a"]), quantise_w("w1", w1, 1, ["stage_b"])]
+        w2_q = [quantise_w("w2", w2, 0, ["stage_c"]), quantise_w("w2", w2, 1, ["stage_a", "stage_b"])]
+
+        def product(jt, wq, passes=(0, 1)):
+            acc = bank(jt)
+            for a in passes:
+                nc.tensor.matmul_mx(
+                    out=acc[:], lhsT=v_words(a, jt), lhsT_scale=v_plane(a, jt), rhs=wq[a][0], rhs_scale=wq[a][1],
+                    start=(a == passes[0]), stop=(a == passes[-1]),
+                )
+            return acc
 
         jts = S // P
-        a3 = [bank(jt) for jt in range(jts)]
-        for a in range(PASSES):
-            plane = v_sc if a == 0 else v_sc_last
-            for jt in range(jts):
-                nc.tensor.matmul_mx(
-                    out=a3[jt][:], lhsT=v_words(a, jt), lhsT_scale=plane[:, P * jt : P * (jt + 1)],
-                    rhs=w3[:, a, :].bitcast(FP4X4), rhs_scale=w3_sc[:, a, :],
-                    start=(a == 0), stop=(a == PASSES - 1),
-                )
-        tanh3 = []
+        a3 = [product(jt, w3_q) for jt in range(jts)]
+        tanh3, a1, top = [], [], []
         for jt in range(jts):
             th = tile("tanh3_%d" % jt, [P, PACK, P], F32)
             nc.scalar.activation(out=th[:], in_=a3[jt][:].rearrange("p (q t) -> p t q", t=PACK), func=ACT.Tanh)
             tanh3.append(th)
-
-        def quantise_w(name, a, raws, slices):
-            grouped = tile("w_bf16", [P, PACK, P, PACK], BF16, bufs=2)
-            qs = P // len(raws)
-            for h, raw in enumerate(raws):
-                nc.vector.tensor_copy(
-                    out=grouped[:, :, qs * h : qs * (h + 1), :].rearrange("p t q j -> p q j t"),
-                    in_=raw[:].rearrange("p j (q t) -> p q j t", t=PACK),
-                )
-            codes = tile("%s_codes%d" % (name, a), [P, H], U32)
-            scales = tile("%s_sc%d" % (name, a), [P, H], U8)
-            ts = PACK // slices
-            for s in range(slices):
-                cols = slice(P * ts * s, P * ts * (s + 1))
-                nc.vector.quantize_mx(
-                    out=codes[:, cols].bitcast(FP8X4), scales=scales[:, cols],
-                    in_=grouped[:, ts * s : ts * (s + 1)].rearrange("p t q j -> p (t q j)"),
-                )
-            return codes, scales
-
-        w1_q = [quantise_w("w1", a, w1_raw[a], 2) for a in range(PASSES)]
-
-        def product(dst, wq, jt0, count, cols):
-            width = BANK // count
-            for a in range(PASSES):
-                for k in range(count):
-                    nc.tensor.matmul_mx(
-                        out=dst[:, width * k : width * (k + 1)],
-                        lhsT=v_words(a, jt0 + k), lhsT_scale=v_plane(a, jt0 + k),
-                        rhs=wq[a][0][:, cols].bitcast(FP8X4), rhs_scale=wq[a][1][:, cols],
-                        start=(a == 0 and k == 0), stop=(a == PASSES - 1 and k == count - 1),
-                    )
-
-        def first_product(u):
-            a1u = tile("a1_%d" % u, [P, 2, jts, P], F32)
-            for jj in range(4):
-                acc = bank(4 * u + jj)
-                product(acc, w1_q, 2 * jj, 2, slice(2 * P * u, 2 * P * (u + 1)))
-                nc.scalar.copy(
-                    out=a1u[:, :, 2 * jj : 2 * jj + 2, :],
-                    in_=acc[:].rearrange("p (k t q) -> p t k q", k=2, t=2),
-                )
-            return a1u
-
-        a1 = first_product(0)
-
-        w2_q = [quantise_w("w2", 0, w2_raw[0], 1), quantise_w("w2", 1, w2_raw[1], 4)]
-
-        w4 = tile("w4", [P, 2, PACK, P], I32)
-        w4_sc = tile("w4_sc", [P, 2, PACK, P], U8)
-
-        def deal_w4():
-            nc.vector.tensor_copy(
-                out=w4[:].rearrange("p g t q -> p g q t"),
-                in_=w4_raw[:].rearrange("p (g q t) -> p g q t", g=2, t=PACK),
+            first = tile("a1_%d" % jt, [P, BANK], F32)
+            nc.scalar.copy(out=first[:], in_=product(jt, w1_q)[:])
+            a1.append(first)
+        for jt in range(jts):
+            larger = tile("top_%d" % jt, [P, PACK, 2, P // 2], F32)
+            nc.vector.tensor_tensor(
+                out=larger[:].rearrange("p t u q -> p u t q"),
+                in0=product(jt, w2_q, (0, 1) if jt < 4 else (1, 0))[:].rearrange("p (u t q) -> p u t q", u=2, t=PACK),
+                in1=a1[jt][:].rearrange("p (u t q) -> p u t q", u=2, t=PACK), op=ALU.max,
             )
-            nc.vector.tensor_copy(
-                out=w4_sc[:].rearrange("p g t q -> p g q t"),
-                in_=w4_sc_raw[:].rearrange("p (g q t) -> p g q t", g=2, t=PACK),
-            )
+            top.append(larger)
 
-        z = [tile("z%d" % h, [P, PACK, M1 // 2], F32) for h in range(2)]
-        for t in range(PACK):
-            if t == 2:
-                a1 = first_product(1)
-            first_bank = 4 if t in (0, 3) else 0
-            h_t = tile("h", [P, S], F32, bufs=3)
-            for h in range(2):
-                acc = bank(first_bank + h)
-                product(acc, w2_q, 4 * h, 4, slice(P * t, P * (t + 1)))
-                top = tile("top", [P, 4, P], F32, bufs=4)
-                nc.vector.tensor_tensor(
-                    out=top[:], in0=acc[:].rearrange("p (k q) -> p k q", k=4),
-                    in1=a1[:, t % 2, 4 * h : 4 * h + 4, :], op=ALU.max,
-                )
-                turned = bank(first_bank + 2 + h)
-                for k in range(4):
-                    cols = slice(P * k, P * (k + 1))
-                    nc.tensor.matmul(turned[:, cols], tanh3[4 * h + k][:, t, :], ident[:],
-                                     start=True, stop=False, is_transpose=True)
-                    nc.tensor.matmul(turned[:, cols], top[:, k, :], ident[:],
-                                     start=False, stop=True, is_transpose=True)
-                nc.scalar.activation(out=h_t[:, BANK * h : BANK * (h + 1)], in_=turned[:], func=ACT.Copy,
-                                     scale=gain_sb[:, t : t + 1])
-            if t == 0:
-                deal_w4()
-            shade = tile("shade", [P, M1], F32, bufs=2)
-            nc.vector.tensor_copy(out=shade[:], in_=h_t[:].indirect(p2[:]))
-            for h in range(2):
-                nc.vector.tensor_tensor(
-                    out=z[h][:, t, :], in0=h_t[:].indirect(p1[:, 16 * h : 16 * (h + 1)]),
-                    in1=shade[:, 256 * h : 256 * (h + 1)], op=ALU.subtract,
-                )
+        w4_raw = tile("stage_c", [P, N], I32)
+        nc.sync.dma_start(out=w4_raw[:], in_=w4_words[0].rearrange("p c i -> p (c i)").bitcast(I32))
+
+        def deal(name, dtype, src):
+            dst = tile(name, [P, 2, PACK, P], dtype)
+            nc.vector.tensor_copy(
+                out=dst[:].rearrange("p g t q -> p g q t"), in_=src.rearrange("p (g q t) -> p g q t", g=2, t=PACK)
+            )
+            return dst
 
         def interleave(copy, name, src):
             width = src.shape[2]
@@ -242,6 +180,37 @@ def tile_list_canopy_berry_walk_kernel(
             copy(out=dst[:].rearrange("p (c i) t -> p c t i", i=4), in_=src[:].rearrange("p t (c i) -> p c t i", i=4))
             return dst
 
+        z = [tile("z%d" % h, [P, PACK, M1 // 2], F32) for h in range(2)]
+        h_banks = ((0, 4), (1, 5), (4, 6), (5, 7))
+        for t in range(PACK):
+            h_t = tile("h", [P, S], F32, bufs=4)
+            for h in range(2):
+                turned = bank(h_banks[t][h])
+                for k in range(4):
+                    nc.tensor.matmul(turned[:, P * k : P * (k + 1)], tanh3[4 * h + k][:, t, :], ident[:],
+                                     start=(k == 0), stop=False, is_transpose=True)
+                for k in range(4):
+                    nc.tensor.matmul(turned[:, P * k : P * (k + 1)],
+                                     top[4 * h + k][:, t].rearrange("p u q -> p (u q)"), ident[:],
+                                     start=False, stop=(k == 3), is_transpose=True)
+                nc.scalar.activation(out=h_t[:, BANK * h : BANK * (h + 1)], in_=turned[:], func=ACT.Copy,
+                                     scale=gain_sb[:, t : t + 1])
+            shade = tile("shade", [P, M1], F32, bufs=2)
+            parts = 2 if t == PACK - 1 else 1
+            for h in range(2):
+                if h < parts:
+                    width = M1 // parts
+                    nc.vector.tensor_copy(
+                        out=shade[:, width * h : width * (h + 1)],
+                        in_=h_t[:].indirect(p2[:, width // 16 * h : width // 16 * (h + 1)]),
+                    )
+                nc.vector.tensor_tensor(
+                    out=z[h][:, t, :], in0=h_t[:].indirect(p1[:, 16 * h : 16 * (h + 1)]),
+                    in1=shade[:, 256 * h : 256 * (h + 1)], op=ALU.subtract,
+                )
+
+        w4 = deal("a1_7", I32, w4_raw[:])
+        w4_sc = deal("a1_6", U8, w4_sc_raw[:, 0, :])
         z_codes = tile("z_codes", [P, M1], U32)
         z_sc = tile("z_sc", [P, M1], U8)
         zb = [interleave(nc.scalar.copy, "zb0", z[0]), interleave(nc.vector.tensor_copy, "zb1", z[1])]

@@ -23,6 +23,7 @@ KP = P * PACK
 PASSES = K // KP
 BANK = 512
 QUADS = 4
+STAGE_A, STAGE_B, STAGE_C, STAGE_D = 0, 8192, 24576, 40960
 
 
 def tile_list_canopy_berry_walk_kernel(
@@ -33,10 +34,14 @@ def tile_list_canopy_berry_walk_kernel(
     with ExitStack() as ctx:
         lists = ctx.enter_context(tc.tile_pool(name="lists", bufs=1))
         sbuf = ctx.enter_context(tc.tile_pool(name="sbuf", bufs=1))
+        staging = ctx.enter_context(tc.tile_pool(name="staging", bufs=1))
         psum = ctx.enter_context(tc.psum_pool(name="psum", bufs=1))
 
         def tile(name, shape, dtype, bufs=1):
             return sbuf.tile(shape, dtype, name=name, bufs=bufs, align_bytes=64)
+
+        def staged(name, offset, shape, dtype):
+            return staging.tile(shape, dtype, name=name, offset=offset, align_bytes=64)
 
         def bank(b):
             return psum.tile([P, BANK], F32, name="bank%d" % b)
@@ -46,27 +51,21 @@ def tile_list_canopy_berry_walk_kernel(
             nc.sync.dma_start(dst[:], src)
             return dst
 
-        w3 = tile("w3", [P, PASSES, 2 * H], U8)
-        nc.sync.dma_start(out=w3[:].bitcast(I32), in_=w3_words.rearrange("a p c -> p a c").bitcast(I32))
         idx = load_list("idx", offs)
+        tab_sc = staged("tab_sc", STAGE_D - T // 2, [P, T], U8)
+        nc.sync.dma_start(out=tab_sc[0:32, :].bitcast(I32), in_=tab_scales.rearrange("a x c -> x a c").bitcast(I32))
+        nc.vector.memset(tab_sc[32:64, :].bitcast(I32), 0)
+        nc.vector.memset(tab_sc[64:P, :].bitcast(I32), 0)
         p1 = load_list("p1", pos1)
         p2 = load_list("p2", pos2)
         p3 = load_list("p3", pos3)
         p4 = load_list("p4", pos4)
-        gain_sb = tile("gain_sb", [P, PACK], F32)
-        nc.sync.dma_start(out=gain_sb[:], in_=gain.rearrange("(p t) -> p t", t=PACK))
-
-        tab_sc = tile("stage_a", [P, T], U8)
-        nc.vector.memset(tab_sc[:].bitcast(I32), 0)
-        nc.scalar.dma_start(
-            out=tab_sc[0:P:4, :].bitcast(I32), in_=tab_scales.rearrange("a x c -> x a c").bitcast(I32)
-        )
         v_sc = tile("v_sc", [P, PASSES, S], U8)
         nc.vector.memset(v_sc[:].bitcast(I32), 0)
 
-        def load_scale_rows(name, src):
+        def load_scale_rows(name, src, clearing_engine):
             dst = tile(name, [P, src.shape[0], src.shape[2]], U8)
-            nc.gpsimd.memset(dst[:].bitcast(I32), 0)
+            clearing_engine.memset(dst[:].bitcast(I32), 0)
             for q in range(QUADS):
                 nc.gpsimd.dma_start(
                     out=dst[32 * q : 32 * q + 4].bitcast(I32),
@@ -74,30 +73,36 @@ def tile_list_canopy_berry_walk_kernel(
                 )
             return dst
 
-        w3_sc = load_scale_rows("w3_sc", w3_scales)
-        w4_sc_raw = load_scale_rows("w4_sc_raw", w4_scales)
+        w3_sc = load_scale_rows("w3_sc", w3_scales, nc.gpsimd)
+        w4_sc_raw = load_scale_rows("w4_sc_raw", w4_scales, nc.vector)
+        gain_sb = tile("gain_sb", [P, PACK], F32)
+        nc.gpsimd.dma_start(out=gain_sb[:], in_=gain.rearrange("(p t) -> p t", t=PACK))
         ident = tile("ident", [P, P], F32)
         make_identity(nc, ident[:])
 
-        tab = []
-        for a, name in enumerate(("stage_b", "stage_c")):
-            words = tile(name, [P, T], I32)
+        def load_tab(a, stage):
+            words = staged("tab%d" % a, stage, [P, T], I32)
             nc.sync.dma_start(out=words[:], in_=tab_words[a].rearrange("p c i -> p (c i)").bitcast(I32))
-            tab.append(words)
+            return words
 
-        picked_sc = tile("picked_sc", [P, S], U8)
+        tab = [load_tab(0, STAGE_B)]
+        w3 = tile("w3", [P, PASSES, 2 * H], U8)
+        nc.sync.dma_start(out=w3[:].bitcast(I32), in_=w3_words.rearrange("a p c -> p a c").bitcast(I32))
+
+        picked_sc = staged("picked_sc", STAGE_A, [P, S], U8)
         nc.vector.tensor_copy(out=picked_sc[:], in_=tab_sc[:].indirect(idx[:]))
         for q in range(QUADS):
             nc.sync.dma_start(
                 out=v_sc[32 * q : 32 * q + 4].bitcast(I32),
-                in_=picked_sc[32 * q : 32 * q + 32 : 4, :].bitcast(I32),
+                in_=picked_sc[8 * q : 8 * q + 8, :].bitcast(I32),
             )
+        tab.append(load_tab(1, STAGE_C))
         half_cols = S // 2 // 16
         v = []
         for a in range(PASSES):
             halves = []
             for h in range(2):
-                vh = tile("v%d_%d" % (a, h), [P, S // 2], U32)
+                vh = staged("v%d_%d" % (a, h), STAGE_D + 2048 * (2 * a + h), [P, S // 2], U32)
                 nc.vector.tensor_copy(
                     out=vh[:], in_=tab[a][:].bitcast(U32).indirect(idx[:, half_cols * h : half_cols * (h + 1)])
                 )
@@ -110,33 +115,41 @@ def tile_list_canopy_berry_walk_kernel(
         def v_plane(a, jt):
             return v_sc[:, a, P * jt : P * (jt + 1)]
 
-        def quantise_w(name, w, a, stages):
+        def quantise_w(name, w, a, stages, second_copy):
             rows = w[KP * a : KP * (a + 1), :].rearrange("(p j) c -> p j c", j=PACK)
-            grouped = tile("w_bf16", [P, 2, PACK, P // 2, PACK], BF16, bufs=2)
             codes = tile("%s_codes%d" % (name, a), [P, H], U32)
             scales = tile("%s_sc%d" % (name, a), [P, H], U8)
             width = H // len(stages)
-            us = 2 // len(stages)
+            raw = []
             for s, stage in enumerate(stages):
-                cols = slice(width * s, width * (s + 1))
-                raw = tile(stage, [P, PACK, width], F32)
-                nc.sync.dma_start(out=raw[:], in_=rows[:, :, cols])
-                part = grouped[:, us * s : us * (s + 1)]
-                nc.vector.tensor_copy(
-                    out=part.rearrange("p u t q j -> p u q j t"),
-                    in_=raw[:].rearrange("p j (u q t) -> p u q j t", u=us, t=PACK),
-                )
+                loaded = staged("%s_raw%d_%d" % (name, a, s), stage, [P, PACK, width], F32)
+                nc.sync.dma_start(out=loaded[:], in_=rows[:, :, width * s : width * (s + 1)])
+                raw.extend(loaded[:, :, c : c + H // 2] for c in range(0, width, H // 2))
+            grouped = []
+            for u, copy in enumerate((nc.vector.tensor_copy, second_copy)):
+                half = tile("w_bf16", [P, PACK, P // 2, PACK], BF16, bufs=4)
+                copy(out=half[:].rearrange("p t q j -> p q j t"), in_=raw[u].rearrange("p j (q t) -> p q j t", t=PACK))
+                grouped.append(half)
+            for u, half in enumerate(grouped):
+                cols = slice(H // 2 * u, H // 2 * (u + 1))
                 nc.vector.quantize_mx(
                     out=codes[:, cols].bitcast(FP8X4), scales=scales[:, cols],
-                    in_=part.rearrange("p u t q j -> p (u t q j)"),
+                    in_=half[:].rearrange("p t q j -> p (t q j)"),
                 )
             return codes[:].bitcast(FP8X4), scales[:]
 
         w3_q = [(w3[:, a, :].bitcast(FP4X4), w3_sc[:, a, :]) for a in range(PASSES)]
-        w1_q = [quantise_w("w1", w1, 0, ["stage_a"]), quantise_w("w1", w1, 1, ["stage_b"])]
-        w2_q = [quantise_w("w2", w2, 0, ["stage_c"]), quantise_w("w2", w2, 1, ["stage_a", "stage_b"])]
+        w1_q = [
+            quantise_w("w1", w1, 0, [STAGE_A], nc.scalar.copy),
+            quantise_w("w1", w1, 1, [STAGE_B], nc.vector.tensor_copy),
+        ]
+        w2_q = [
+            quantise_w("w2", w2, 0, [STAGE_C], nc.vector.tensor_copy),
+            quantise_w("w2", w2, 1, [STAGE_A, STAGE_B], nc.vector.tensor_copy),
+        ]
 
-        def product(jt, wq, passes=(0, 1)):
+        def product(jt, wq):
+            passes = (0, 1) if jt < 4 else (1, 0)
             acc = bank(jt)
             for a in passes:
                 nc.tensor.matmul_mx(
@@ -159,12 +172,12 @@ def tile_list_canopy_berry_walk_kernel(
             larger = tile("top_%d" % jt, [P, PACK, 2, P // 2], F32)
             nc.vector.tensor_tensor(
                 out=larger[:].rearrange("p t u q -> p u t q"),
-                in0=product(jt, w2_q, (0, 1) if jt < 4 else (1, 0))[:].rearrange("p (u t q) -> p u t q", u=2, t=PACK),
+                in0=product(jt, w2_q)[:].rearrange("p (u t q) -> p u t q", u=2, t=PACK),
                 in1=a1[jt][:].rearrange("p (u t q) -> p u t q", u=2, t=PACK), op=ALU.max,
             )
             top.append(larger)
 
-        w4_raw = tile("stage_c", [P, N], I32)
+        w4_raw = staged("w4_raw", STAGE_C, [P, N], I32)
         nc.sync.dma_start(out=w4_raw[:], in_=w4_words[0].rearrange("p c i -> p (c i)").bitcast(I32))
 
         def deal(name, dtype, src):
@@ -177,7 +190,7 @@ def tile_list_canopy_berry_walk_kernel(
         def interleave(copy, name, src):
             width = src.shape[2]
             dst = tile(name, [P, width, PACK], BF16)
-            copy(out=dst[:].rearrange("p (c i) t -> p c t i", i=4), in_=src[:].rearrange("p t (c i) -> p c t i", i=4))
+            copy(out=dst[:].rearrange("p (c i) t -> p c t i", i=4), in_=src.rearrange("p t (c i) -> p c t i", i=4))
             return dst
 
         z = [tile("z%d" % h, [P, PACK, M1 // 2], F32) for h in range(2)]
@@ -195,54 +208,69 @@ def tile_list_canopy_berry_walk_kernel(
                                      start=False, stop=(k == 3), is_transpose=True)
                 nc.scalar.activation(out=h_t[:, BANK * h : BANK * (h + 1)], in_=turned[:], func=ACT.Copy,
                                      scale=gain_sb[:, t : t + 1])
-            shade = tile("shade", [P, M1], F32, bufs=2)
-            parts = 2 if t == PACK - 1 else 1
+            shade = []
             for h in range(2):
-                if h < parts:
-                    width = M1 // parts
-                    nc.vector.tensor_copy(
-                        out=shade[:, width * h : width * (h + 1)],
-                        in_=h_t[:].indirect(p2[:, width // 16 * h : width // 16 * (h + 1)]),
-                    )
+                picked = tile("shade", [P, M1 // 2], F32, bufs=4)
+                nc.vector.tensor_copy(out=picked[:], in_=h_t[:].indirect(p2[:, 16 * h : 16 * (h + 1)]))
+                shade.append(picked)
+            for h in range(2):
                 nc.vector.tensor_tensor(
                     out=z[h][:, t, :], in0=h_t[:].indirect(p1[:, 16 * h : 16 * (h + 1)]),
-                    in1=shade[:, 256 * h : 256 * (h + 1)], op=ALU.subtract,
+                    in1=shade[h][:], op=ALU.subtract,
                 )
 
         w4 = deal("a1_7", I32, w4_raw[:])
         w4_sc = deal("a1_6", U8, w4_sc_raw[:, 0, :])
         z_codes = tile("z_codes", [P, M1], U32)
         z_sc = tile("z_sc", [P, M1], U8)
-        zb = [interleave(nc.scalar.copy, "zb0", z[0]), interleave(nc.vector.tensor_copy, "zb1", z[1])]
+        zb = [interleave(nc.scalar.copy, "zb0", z[0][:]), interleave(nc.vector.tensor_copy, "zb1", z[1][:])]
         for h in range(2):
             cols = slice(256 * h, 256 * (h + 1))
             nc.vector.quantize_mx(out=z_codes[:, cols].bitcast(FP8X4), scales=z_sc[:, cols],
                                   in_=zb[h][:].rearrange("p m t -> p (m t)"))
 
         y_rows = out_0.rearrange("(g p t) j -> g p t j", g=2, t=PACK)
+        y = [tile("y%d" % g, [P, PACK, M2], F32) for g in range(2)]
+        y_codes = [tile("y_codes%d" % g, [P, M2], I32) for g in range(2)]
         y_sc = tile("y_sc", [P, 2, M2], U8)
+        halves = [slice(M2 // 2 * s, M2 // 2 * (s + 1)) for s in range(2)]
+
+        def quantise_y(g, cols, rounded):
+            nc.vector.quantize_mx(out=y_codes[g][:, cols].bitcast(FP8X4), scales=y_sc[:, g, cols],
+                                  in_=rounded[:].rearrange("p m t -> p (m t)"))
+
+        def store_codes(g):
+            nc.sync.dma_start(out=out_1[g].rearrange("p m i -> p (m i)").bitcast(I32), in_=y_codes[g][:])
+
         for g in range(2):
-            y = tile("y%d" % g, [P, PACK, M2], F32)
             for t in range(PACK):
-                acc = bank(4 * g + t)
-                nc.tensor.matmul_mx(
-                    out=acc[:], lhsT=w4[:, g, t, :].bitcast(FP8X4), lhsT_scale=w4_sc[:, g, t, :],
-                    rhs=z_codes[:].bitcast(FP8X4), rhs_scale=z_sc[:], start=True, stop=True,
-                )
-                f = tile("f", [P, M1], F32, bufs=4)
-                nc.scalar.copy(out=f[:], in_=acc[:])
-                other = tile("other", [P, M2], F32, bufs=3)
+                f = tile("f", [P, M1], F32, bufs=8)
+                parts = 2 if (g, t) == (0, 0) else 1
+                for s in range(parts):
+                    cols = slice(M1 // parts * s, M1 // parts * (s + 1))
+                    acc = bank((4 * g + t - s) % 8)
+                    nc.tensor.matmul_mx(
+                        out=acc[:, cols], lhsT=w4[:, g, t, :].bitcast(FP8X4), lhsT_scale=w4_sc[:, g, t, :],
+                        rhs=z_codes[:, cols].bitcast(FP8X4), rhs_scale=z_sc[:, cols], start=True, stop=True,
+                    )
+                    nc.scalar.copy(out=f[:, cols], in_=acc[:, cols])
+                other = tile("other", [P, M2], F32, bufs=4)
                 nc.vector.tensor_copy(out=other[:], in_=f[:].indirect(p4[:]))
-                bounded = tile("bounded", [P, M2], F32, bufs=3)
+                bounded = tile("bounded", [P, M2], F32, bufs=4)
                 nc.scalar.activation(out=bounded[:], in_=other[:], func=ACT.Tanh)
-                nc.vector.tensor_tensor(out=y[:, t, :], in0=f[:].indirect(p3[:]), in1=bounded[:], op=ALU.mult)
-                if t % 2 == 1:
-                    nc.sync.dma_start(out=y_rows[g, :, t - 1 : t + 1, :], in_=y[:, t - 1 : t + 1, :])
-            yb = interleave(nc.scalar.copy if g == 0 else nc.vector.tensor_copy, "yb%d" % g, y)
-            y_codes = tile("y_codes%d" % g, [P, M2], I32)
-            nc.vector.quantize_mx(out=y_codes[:].bitcast(FP8X4), scales=y_sc[:, g, :],
-                                  in_=yb[:].rearrange("p m t -> p (m t)"))
-            nc.sync.dma_start(out=out_1[g].rearrange("p m i -> p (m i)").bitcast(I32), in_=y_codes[:])
+                for cols in halves if (g, t) == (1, PACK - 1) else [slice(0, M2)]:
+                    nc.vector.tensor_tensor(
+                        out=y[g][:, t, cols], in0=f[:].indirect(p3[:, cols.start // 16 : cols.stop // 16]),
+                        in1=bounded[:, cols], op=ALU.mult,
+                    )
+                nc.sync.dma_start(out=y_rows[g, :, t, :], in_=y[g][:, t, :])
+                if g == 1 and t < 2:
+                    quantise_y(0, halves[t], interleave(nc.scalar.copy, "yb0_%d" % t, y[0][:, :, halves[t]]))
+        store_codes(0)
+        rounded = [interleave(nc.vector.tensor_copy, "yb1_%d" % s, y[1][:, :, halves[s]]) for s in range(2)]
+        for s in range(2):
+            quantise_y(1, halves[s], rounded[s])
+        store_codes(1)
         for q in range(QUADS):
             queue = nc.scalar if q % 2 == 0 else nc.sync
             queue.dma_start(

from contextlib import ExitStack

import concourse.mybir as mybir
from concourse.masks import make_identity

K, H, N, T, S, M1, M2 = 1024, 512, 1024, 4096, 1024, 512, 256
FLOPS = 2 * (3 * K * H * S + H * N * M1)

F32 = mybir.dt.float32
BF16 = mybir.dt.bfloat16
I32 = mybir.dt.int32
U32 = mybir.dt.uint32
U16 = mybir.dt.uint16
U8 = mybir.dt.uint8
FP8X4 = mybir.dt.float8_e4m3fn_x4
FP4X4 = mybir.dt.float4_e2m1fn_x4
ALU = mybir.AluOpType
ACT = mybir.ActivationFunctionType

P = 128
PACK = 4
KP = P * PACK
PASSES = K // KP
BANK = 512
QUADS = 4
STAGE_A, STAGE_B, STAGE_C, STAGE_D = 0, 8192, 24576, 40960


def tile_list_canopy_berry_walk_kernel(
    tc, tab_words, tab_scales, offs, w1, w2, w3_words, w3_scales, gain,
    pos1, pos2, w4_words, w4_scales, pos3, pos4, out_0, out_1, out_2,
):
    nc = tc.nc
    with ExitStack() as ctx:
        lists = ctx.enter_context(tc.tile_pool(name="lists", bufs=1))
        sbuf = ctx.enter_context(tc.tile_pool(name="sbuf", bufs=1))
        staging = ctx.enter_context(tc.tile_pool(name="staging", bufs=1))
        psum = ctx.enter_context(tc.psum_pool(name="psum", bufs=1))

        def tile(name, shape, dtype, bufs=1):
            return sbuf.tile(shape, dtype, name=name, bufs=bufs, align_bytes=64)

        def staged(name, offset, shape, dtype):
            return staging.tile(shape, dtype, name=name, offset=offset, align_bytes=64)

        def bank(b):
            return psum.tile([P, BANK], F32, name="bank%d" % b)

        def load_list(name, src):
            dst = lists.tile(list(src.shape), U16, name=name)
            nc.sync.dma_start(dst[:], src)
            return dst

        idx = load_list("idx", offs)
        tab_sc = staged("tab_sc", STAGE_D - T // 2, [P, T], U8)
        nc.sync.dma_start(out=tab_sc[0:32, :].bitcast(I32), in_=tab_scales.rearrange("a x c -> x a c").bitcast(I32))
        nc.vector.memset(tab_sc[32:64, :].bitcast(I32), 0)
        nc.vector.memset(tab_sc[64:P, :].bitcast(I32), 0)
        p1 = load_list("p1", pos1)
        p2 = load_list("p2", pos2)
        p3 = load_list("p3", pos3)
        p4 = load_list("p4", pos4)
        v_sc = tile("v_sc", [P, PASSES, S], U8)
        nc.vector.memset(v_sc[:].bitcast(I32), 0)

        def load_scale_rows(name, src, clearing_engine):
            dst = tile(name, [P, src.shape[0], src.shape[2]], U8)
            clearing_engine.memset(dst[:].bitcast(I32), 0)
            for q in range(QUADS):
                nc.gpsimd.dma_start(
                    out=dst[32 * q : 32 * q + 4].bitcast(I32),
                    in_=src[:, 4 * q : 4 * q + 4, :].rearrange("a r c -> r a c").bitcast(I32),
                )
            return dst

        w3_sc = load_scale_rows("w3_sc", w3_scales, nc.gpsimd)
        w4_sc_raw = load_scale_rows("w4_sc_raw", w4_scales, nc.vector)
        gain_sb = tile("gain_sb", [P, PACK], F32)
        nc.gpsimd.dma_start(out=gain_sb[:], in_=gain.rearrange("(p t) -> p t", t=PACK))
        ident = tile("ident", [P, P], F32)
        make_identity(nc, ident[:])

        def load_tab(a, stage):
            words = staged("tab%d" % a, stage, [P, T], I32)
            nc.sync.dma_start(out=words[:], in_=tab_words[a].rearrange("p c i -> p (c i)").bitcast(I32))
            return words

        tab = [load_tab(0, STAGE_B)]
        w3 = tile("w3", [P, PASSES, 2 * H], U8)
        nc.sync.dma_start(out=w3[:].bitcast(I32), in_=w3_words.rearrange("a p c -> p a c").bitcast(I32))

        picked_sc = staged("picked_sc", STAGE_A, [P, S], U8)
        nc.vector.tensor_copy(out=picked_sc[:], in_=tab_sc[:].indirect(idx[:]))
        for q in range(QUADS):
            nc.sync.dma_start(
                out=v_sc[32 * q : 32 * q + 4].bitcast(I32),
                in_=picked_sc[8 * q : 8 * q + 8, :].bitcast(I32),
            )
        tab.append(load_tab(1, STAGE_C))
        half_cols = S // 2 // 16
        v = []
        for a in range(PASSES):
            halves = []
            for h in range(2):
                vh = staged("v%d_%d" % (a, h), STAGE_D + 2048 * (2 * a + h), [P, S // 2], U32)
                nc.vector.tensor_copy(
                    out=vh[:], in_=tab[a][:].bitcast(U32).indirect(idx[:, half_cols * h : half_cols * (h + 1)])
                )
                halves.append(vh)
            v.append(halves)

        def v_words(a, jt):
            return v[a][jt // 4][:, P * (jt % 4) : P * (jt % 4 + 1)].bitcast(FP8X4)

        def v_plane(a, jt):
            return v_sc[:, a, P * jt : P * (jt + 1)]

        def quantise_w(name, w, a, stages, second_copy):
            rows = w[KP * a : KP * (a + 1), :].rearrange("(p j) c -> p j c", j=PACK)
            codes = tile("%s_codes%d" % (name, a), [P, H], U32)
            scales = tile("%s_sc%d" % (name, a), [P, H], U8)
            width = H // len(stages)
            raw = []
            for s, stage in enumerate(stages):
                loaded = staged("%s_raw%d_%d" % (name, a, s), stage, [P, PACK, width], F32)
                nc.sync.dma_start(out=loaded[:], in_=rows[:, :, width * s : width * (s + 1)])
                raw.extend(loaded[:, :, c : c + H // 2] for c in range(0, width, H // 2))
            grouped = []
            for u, copy in enumerate((nc.vector.tensor_copy, second_copy)):
                half = tile("w_bf16", [P, PACK, P // 2, PACK], BF16, bufs=4)
                copy(out=half[:].rearrange("p t q j -> p q j t"), in_=raw[u].rearrange("p j (q t) -> p q j t", t=PACK))
                grouped.append(half)
            for u, half in enumerate(grouped):
                cols = slice(H // 2 * u, H // 2 * (u + 1))
                nc.vector.quantize_mx(
                    out=codes[:, cols].bitcast(FP8X4), scales=scales[:, cols],
                    in_=half[:].rearrange("p t q j -> p (t q j)"),
                )
            return codes[:].bitcast(FP8X4), scales[:]

        w3_q = [(w3[:, a, :].bitcast(FP4X4), w3_sc[:, a, :]) for a in range(PASSES)]
        w1_q = [
            quantise_w("w1", w1, 0, [STAGE_A], nc.scalar.copy),
            quantise_w("w1", w1, 1, [STAGE_B], nc.vector.tensor_copy),
        ]
        w2_q = [
            quantise_w("w2", w2, 0, [STAGE_C], nc.vector.tensor_copy),
            quantise_w("w2", w2, 1, [STAGE_A, STAGE_B], nc.vector.tensor_copy),
        ]

        def product(jt, wq):
            passes = (0, 1) if jt < 4 else (1, 0)
            acc = bank(jt)
            for a in passes:
                nc.tensor.matmul_mx(
                    out=acc[:], lhsT=v_words(a, jt), lhsT_scale=v_plane(a, jt), rhs=wq[a][0], rhs_scale=wq[a][1],
                    start=(a == passes[0]), stop=(a == passes[-1]),
                )
            return acc

        jts = S // P
        a3 = [product(jt, w3_q) for jt in range(jts)]
        tanh3, a1, top = [], [], []
        for jt in range(jts):
            th = tile("tanh3_%d" % jt, [P, PACK, P], F32)
            nc.scalar.activation(out=th[:], in_=a3[jt][:].rearrange("p (q t) -> p t q", t=PACK), func=ACT.Tanh)
            tanh3.append(th)
            first = tile("a1_%d" % jt, [P, BANK], F32)
            nc.scalar.copy(out=first[:], in_=product(jt, w1_q)[:])
            a1.append(first)
        for jt in range(jts):
            larger = tile("top_%d" % jt, [P, PACK, 2, P // 2], F32)
            nc.vector.tensor_tensor(
                out=larger[:].rearrange("p t u q -> p u t q"),
                in0=product(jt, w2_q)[:].rearrange("p (u t q) -> p u t q", u=2, t=PACK),
                in1=a1[jt][:].rearrange("p (u t q) -> p u t q", u=2, t=PACK), op=ALU.max,
            )
            top.append(larger)

        w4_raw = staged("w4_raw", STAGE_C, [P, N], I32)
        nc.sync.dma_start(out=w4_raw[:], in_=w4_words[0].rearrange("p c i -> p (c i)").bitcast(I32))

        def deal(name, dtype, src):
            dst = tile(name, [P, 2, PACK, P], dtype)
            nc.vector.tensor_copy(
                out=dst[:].rearrange("p g t q -> p g q t"), in_=src.rearrange("p (g q t) -> p g q t", g=2, t=PACK)
            )
            return dst

        def interleave(copy, name, src):
            width = src.shape[2]
            dst = tile(name, [P, width, PACK], BF16)
            copy(out=dst[:].rearrange("p (c i) t -> p c t i", i=4), in_=src.rearrange("p t (c i) -> p c t i", i=4))
            return dst

        z = [tile("z%d" % h, [P, PACK, M1 // 2], F32) for h in range(2)]
        h_banks = ((0, 4), (1, 5), (4, 6), (5, 7))
        for t in range(PACK):
            h_t = tile("h", [P, S], F32, bufs=4)
            for h in range(2):
                turned = bank(h_banks[t][h])
                for k in range(4):
                    nc.tensor.matmul(turned[:, P * k : P * (k + 1)], tanh3[4 * h + k][:, t, :], ident[:],
                                     start=(k == 0), stop=False, is_transpose=True)
                for k in range(4):
                    nc.tensor.matmul(turned[:, P * k : P * (k + 1)],
                                     top[4 * h + k][:, t].rearrange("p u q -> p (u q)"), ident[:],
                                     start=False, stop=(k == 3), is_transpose=True)
                nc.scalar.activation(out=h_t[:, BANK * h : BANK * (h + 1)], in_=turned[:], func=ACT.Copy,
                                     scale=gain_sb[:, t : t + 1])
            shade = []
            for h in range(2):
                picked = tile("shade", [P, M1 // 2], F32, bufs=4)
                nc.vector.tensor_copy(out=picked[:], in_=h_t[:].indirect(p2[:, 16 * h : 16 * (h + 1)]))
                shade.append(picked)
            for h in range(2):
                nc.vector.tensor_tensor(
                    out=z[h][:, t, :], in0=h_t[:].indirect(p1[:, 16 * h : 16 * (h + 1)]),
                    in1=shade[h][:], op=ALU.subtract,
                )

        w4 = deal("a1_7", I32, w4_raw[:])
        w4_sc = deal("a1_6", U8, w4_sc_raw[:, 0, :])
        z_codes = tile("z_codes", [P, M1], U32)
        z_sc = tile("z_sc", [P, M1], U8)
        zb = [interleave(nc.scalar.copy, "zb0", z[0][:]), interleave(nc.vector.tensor_copy, "zb1", z[1][:])]
        for h in range(2):
            cols = slice(256 * h, 256 * (h + 1))
            nc.vector.quantize_mx(out=z_codes[:, cols].bitcast(FP8X4), scales=z_sc[:, cols],
                                  in_=zb[h][:].rearrange("p m t -> p (m t)"))

        y_rows = out_0.rearrange("(g p t) j -> g p t j", g=2, t=PACK)
        y = [tile("y%d" % g, [P, PACK, M2], F32) for g in range(2)]
        y_codes = [tile("y_codes%d" % g, [P, M2], I32) for g in range(2)]
        y_sc = tile("y_sc", [P, 2, M2], U8)
        halves = [slice(M2 // 2 * s, M2 // 2 * (s + 1)) for s in range(2)]

        def quantise_y(g, cols, rounded):
            nc.vector.quantize_mx(out=y_codes[g][:, cols].bitcast(FP8X4), scales=y_sc[:, g, cols],
                                  in_=rounded[:].rearrange("p m t -> p (m t)"))

        def store_codes(g):
            nc.sync.dma_start(out=out_1[g].rearrange("p m i -> p (m i)").bitcast(I32), in_=y_codes[g][:])

        for g in range(2):
            for t in range(PACK):
                f = tile("f", [P, M1], F32, bufs=8)
                parts = 2 if (g, t) == (0, 0) else 1
                for s in range(parts):
                    cols = slice(M1 // parts * s, M1 // parts * (s + 1))
                    acc = bank((4 * g + t - s) % 8)
                    nc.tensor.matmul_mx(
                        out=acc[:, cols], lhsT=w4[:, g, t, :].bitcast(FP8X4), lhsT_scale=w4_sc[:, g, t, :],
                        rhs=z_codes[:, cols].bitcast(FP8X4), rhs_scale=z_sc[:, cols], start=True, stop=True,
                    )
                    nc.scalar.copy(out=f[:, cols], in_=acc[:, cols])
                other = tile("other", [P, M2], F32, bufs=4)
                nc.vector.tensor_copy(out=other[:], in_=f[:].indirect(p4[:]))
                bounded = tile("bounded", [P, M2], F32, bufs=4)
                nc.scalar.activation(out=bounded[:], in_=other[:], func=ACT.Tanh)
                for cols in halves if (g, t) == (1, PACK - 1) else [slice(0, M2)]:
                    nc.vector.tensor_tensor(
                        out=y[g][:, t, cols], in0=f[:].indirect(p3[:, cols.start // 16 : cols.stop // 16]),
                        in1=bounded[:, cols], op=ALU.mult,
                    )
                nc.sync.dma_start(out=y_rows[g, :, t, :], in_=y[g][:, t, :])
                if g == 1 and t < 2:
                    quantise_y(0, halves[t], interleave(nc.scalar.copy, "yb0_%d" % t, y[0][:, :, halves[t]]))
        store_codes(0)
        rounded = [interleave(nc.vector.tensor_copy, "yb1_%d" % s, y[1][:, :, halves[s]]) for s in range(2)]
        for s in range(2):
            quantise_y(1, halves[s], rounded[s])
        store_codes(1)
        for q in range(QUADS):
            queue = nc.scalar if q % 2 == 0 else nc.sync
            queue.dma_start(
                out=out_2[:, 4 * q : 4 * q + 4, :].rearrange("g r m -> r g m").bitcast(I32),
                in_=y_sc[32 * q : 32 * q + 4].bitcast(I32),
            )
